import numpy as np
import ml_dtypes


def mxq(x, axis, fmt="e4m3"):
    dtype, down = {"e4m3": (ml_dtypes.float8_e4m3fn, 7), "e5m2": (ml_dtypes.float8_e5m2, 14)}[fmt]
    v = np.moveaxis(np.asarray(x, np.float32).astype(ml_dtypes.bfloat16).astype(np.float64), axis, -1)
    blocks = v.reshape(v.shape[:-1] + (-1, 32))
    amax = np.abs(blocks).max(-1, keepdims=True)
    byte = np.maximum(np.where(amax > 0, np.frexp(amax)[1] - 1 + 127, 0) - down, 1)
    scale = np.exp2(byte - 127.0)
    codes = (blocks / scale).astype(np.float32).astype(dtype).astype(np.float64)
    return np.moveaxis((codes * scale).reshape(v.shape), -1, axis)


WIDE = False


def mx_kscale(k):
    if not WIDE:
        return np.ones(k)
    levels = np.array([10, -10, 5, -5, 0])
    if k % 512:
        return np.exp2(np.random.permutation(np.resize(levels, k // 32))).repeat(32)
    a = np.empty((k // 512, 16))
    for p in range(k // 512):
        a[p, :8] = np.random.permutation(np.resize(levels, 8))
        for g in range(8):
            far = levels[np.abs(levels - a[p, g]) >= 10]
            a[p, g + 8] = far[np.random.randint(len(far))]
    return np.exp2(a.ravel()).repeat(32)


def f64(x):
    return np.asarray(x).astype(np.float64)


def striped(idx):
    return np.tile(idx.reshape(-1, 16).T, (8, 1)).astype(np.uint16)


def unstriped(offs):
    return offs[:16].T.reshape(-1).astype(np.int64)


def striped8(idx):
    return np.concatenate([x.reshape(-1, 16).T for x in idx]).astype(np.uint16)


def runs(offs, k):
    lists = np.stack([offs[16 * r : 16 * r + 16].T.reshape(-1) for r in range(8)]).astype(np.int64)
    return lists[np.arange(k) % 512 // 64]


def pack_weight(w):
    k, n = w.shape
    w = f64(np.asarray(w, np.float32).astype(ml_dtypes.bfloat16)).reshape(k // 32, 32, n)
    amax = np.abs(w).max(1)
    byte = np.clip(np.where(amax > 0, np.frexp(amax)[1] - 1 + 127 - 7, 1), 1, 254)
    scaled = (w * np.exp2(127.0 - byte)[:, None, :]).reshape(k, n).astype(np.float32)
    words = np.ascontiguousarray(scaled.reshape(k // 512, 128, 4, n).transpose(0, 1, 3, 2)).astype(ml_dtypes.float8_e4m3fn).view(np.uint8)
    return words, np.ascontiguousarray(byte.astype(np.uint8).reshape(k // 512, 16, n))


def unpack_weight(words, scales):
    g, p, n, _ = words.shape
    vals = np.ascontiguousarray(words).view(ml_dtypes.float8_e4m3fn).astype(np.float64) * np.repeat(np.exp2(scales.astype(np.float64) - 127.0), 8, axis=1)[..., None]
    return vals.transpose(0, 1, 3, 2).reshape(g * 512, n)


E2M1 = np.array([0.0, 0.5, 1.0, 1.5, 2.0, 3.0, 4.0, 6.0, -0.0, -0.5, -1.0, -1.5, -2.0, -3.0, -4.0, -6.0])


def pack_fp4(w):
    k, n = w.shape
    w = f64(np.asarray(w, np.float32).astype(ml_dtypes.bfloat16)).reshape(k // 32, 32, n)
    amax = np.abs(w).max(1)
    mant, ex = np.frexp(amax / 6.0)
    byte = np.clip(np.where(amax > 0, np.where(mant > 0.5, ex, ex - 1) + 127, 1), 1, 254)
    scaled = (w * np.exp2(127.0 - byte)[:, None, :]).reshape(k, n).astype(np.float32)
    c = np.ascontiguousarray(scaled.reshape(k // 512, 128, 4, n).transpose(0, 1, 3, 2)).astype(ml_dtypes.float4_e2m1fn).view(np.uint8) & 0xF
    words = (c[..., 0::2] | (c[..., 1::2] << 4)).reshape(k // 512, 128, 2 * n)
    return np.ascontiguousarray(words), np.ascontiguousarray(byte.astype(np.uint8).reshape(k // 512, 16, n))


def unpack_fp4(words, scales):
    g, _, n = scales.shape
    words = np.ascontiguousarray(words).reshape(g, 128, n, 2)
    nib = np.empty((g, 128, n, 4), np.uint8)
    nib[..., 0::2] = words & 0xF
    nib[..., 1::2] = words >> 4
    vals = E2M1[nib] * np.repeat(np.exp2(scales.astype(np.float64) - 127.0), 8, axis=1)[..., None]
    return vals.transpose(0, 1, 3, 2).reshape(g * 512, n)


def planes(y):
    n, m = y.shape
    v = y.astype(np.float32).astype(ml_dtypes.bfloat16).astype(np.float64).reshape(n // 32, 32, m)
    top = np.abs(v).max(1)
    byte = np.clip(np.where(top > 0, np.frexp(top)[1] - 1 + 127 - 7, 1), 1, 254)
    codes = (v * np.exp2(127.0 - byte)[:, None, :]).reshape(n, m).astype(np.float32).astype(ml_dtypes.float8_e4m3fn).view(np.uint8)
    words = codes.reshape(n // 512, 128, 4, m).transpose(0, 1, 3, 2)
    return np.ascontiguousarray(words), np.ascontiguousarray(byte.astype(np.uint8).reshape(n // 512, 16, m))


K, T, S, N, H, W, G = 512, 2048, 512, 512, 512, 256, 384


def setup_inputs():
    n = np.random.standard_normal
    s = mx_kscale(K)[:, None]
    u = mx_kscale(H)
    packed_xT = pack_weight(n((K, T)) * s)
    packed_w1 = pack_fp4(n((K, H)) / np.sqrt(K) / s)
    packed_w2 = pack_fp4(n((H, N)) / np.sqrt(2 * H) / u[:, None])
    packed_w3 = pack_fp4(n((K, N)) / np.sqrt(2 * K) / s)
    perm = np.stack([np.random.permutation(S) for _ in range(8)])
    return {
        "x_words": packed_xT[0],
        "x_scales": packed_xT[1],
        "w1_words": packed_w1[0],
        "w1_scales": packed_w1[1],
        "gn": (np.random.uniform(0.5, 1.5, (H, 1)) * u[:, None]).astype(np.float32),
        "w2_words": packed_w2[0],
        "w2_scales": packed_w2[1],
        "w3_words": packed_w3[0],
        "w3_scales": packed_w3[1],
        "offs": striped(np.random.permutation(T)[:S]),
        "n1": striped8(perm[:, :W]),
        "n2": striped8(perm[:, W:]),
        "hz": striped8(np.random.randint(0, T, (8, S))),
        "n3": striped(np.random.permutation(S)[:G]),
        "n4": striped(np.random.permutation(S)[:G]),
    }


def reference(x_words, x_scales, w1_words, w1_scales, gn, w2_words, w2_scales, w3_words, w3_scales, offs, n1, n2, hz, n3, n4):
    xq = unpack_weight(x_words, x_scales)[:, unstriped(offs)]
    y = unpack_fp4(w1_words, w1_scales).T @ xq
    pa = y[np.arange(H)[:, None], runs(n1, H)]
    pb = y[np.arange(H)[:, None], runs(n2, H)]
    rb = pa - pb
    ra = 0.75 * (pa + pb)
    ds = np.zeros((H, S))
    ds[np.arange(H)[:, None], runs(n1, H)] = ra
    dt = ds.copy()
    dt[np.arange(H)[:, None], runs(n2, H)] = rb
    z = f64(gn) * dt
    x_hz = unpack_weight(x_words, x_scales)[np.arange(K)[:, None], runs(hz, K)]
    h = unpack_fp4(w2_words, w2_scales).T @ mxq(z, 0, "e4m3") + unpack_fp4(w3_words, w3_scales).T @ x_hz
    old = h[:, unstriped(n3)]
    pa2 = h[:, unstriped(n4)]
    ra2 = old / (np.abs(pa2) + 0.5)
    out = h.copy()
    out[:, unstriped(n3)] = ra2
    return (out,) + planes(out)

@@ -1,0 +1,209 @@
+from contextlib import ExitStack
+
+import concourse.mybir as mybir
+
+K, T, S, N, H, W, G = 512, 2048, 512, 512, 512, 256, 384
+FLOPS = 3 * 2 * 512 * 512 * 512
+
+F32 = mybir.dt.float32
+BF16 = mybir.dt.bfloat16
+I32 = mybir.dt.int32
+U32 = mybir.dt.uint32
+U16 = mybir.dt.uint16
+U8 = mybir.dt.uint8
+FP8X4 = mybir.dt.float8_e4m3fn_x4
+FP4X4 = mybir.dt.float4_e2m1fn_x4
+ACT = mybir.ActivationFunctionType
+ALU = mybir.AluOpType
+
+P = 128
+PACK = 4
+
+
+def tile_picked_mixhhaarknorm_none_po_kernel(
+    tc, x_words, x_scales, w1_words, w1_scales, gn, w2_words, w2_scales, w3_words, w3_scales,
+    offs, n1, n2, hz, n3, n4, out_0, out_1, out_2,
+):
+    nc = tc.nc
+    with ExitStack() as ctx:
+        lists = ctx.enter_context(tc.tile_pool(name="lists", bufs=1))
+        sb = ctx.enter_context(tc.tile_pool(name="sb", bufs=1))
+        psum = ctx.enter_context(tc.psum_pool(name="psum", bufs=1))
+
+        def load_list(name, dram):
+            tile = lists.tile(list(dram.shape), U16, name=name)
+            nc.sync.dma_start(tile[:], dram)
+            return tile
+
+        def load_scale_rows(queue, plane, dram):
+            rows = dram[0].bitcast(I32)
+            for j in range(4):
+                queue.dma_start(plane.bitcast(I32)[j:P:32, :], rows[j:16:4, :])
+
+        def deal_words(dealt, raw):
+            nc.vector.tensor_copy(
+                out=dealt.bitcast(U16).rearrange("p (t m) -> p t m", t=PACK),
+                in_=raw.bitcast(U16).rearrange("p (m t) -> p t m", t=PACK),
+            )
+
+        def deal_scales(dealt, raw):
+            nc.vector.tensor_copy(
+                out=dealt.rearrange("p (t m) -> p t m", t=PACK),
+                in_=raw.rearrange("p (m t) -> p t m", t=PACK),
+            )
+
+        def interleave(engine_copy, grouped, planes, c0, c1):
+            engine_copy(
+                out=grouped[:, c0:c1, :].rearrange("p (c i) t -> p c t i", i=4),
+                in_=planes[:, :, c0:c1].rearrange("p t (c i) -> p c t i", i=4),
+            )
+
+        x_bytes = sb.tile([P, T], U8, name="x_bytes", align_bytes=64)
+        nc.vector.memset(x_bytes[:].bitcast(I32), 0)
+        raw_s = [sb.tile([P, N], U8, name=f"raw_s{i}", tag=f"raw_s{i}", align_bytes=64) for i in range(3)]
+        nc.vector.memset(raw_s[0][:].bitcast(I32), 0)
+        run_bytes = sb.tile([P, T], U8, name="run_bytes", align_bytes=64)
+        nc.gpsimd.memset(run_bytes[:].bitcast(I32), 0)
+        for i in (2, 1):
+            nc.gpsimd.memset(raw_s[i][:].bitcast(I32), 0)
+        hz_scales = sb.tile([P, S], U8, name="hz_scales", align_bytes=64)
+        nc.gpsimd.memset(hz_scales[:].bitcast(I32), 0)
+        half = sb.tile([P, 1], F32, name="half")
+        nc.gpsimd.memset(half[:], 0.5)
+
+        load_scale_rows(nc.sync, x_bytes[:], x_scales)
+        offs_t = load_list("offs_t", offs)
+        raw_w = [sb.tile([P, 2 * N], U8, name=f"raw_w{i}", align_bytes=64) for i in range(3)]
+        nc.sync.dma_start(raw_w[0][:].bitcast(I32), w1_words[0].bitcast(I32))
+        hz_t = load_list("hz_t", hz)
+        x_codes = sb.tile([P, T], U32, name="x_codes", align_bytes=64)
+        nc.sync.dma_start(x_codes[:].bitcast(I32), x_words[0].rearrange("p c r -> p (c r)").bitcast(I32))
+        load_scale_rows(nc.sync, raw_s[0][:], w1_scales)
+        gain = sb.tile([P, PACK], F32, name="gain")
+        nc.sync.dma_start(gain[:], gn.rearrange("(p t) o -> p (t o)", t=PACK))
+        n1_t = load_list("n1_t", n1)
+        n2_t = load_list("n2_t", n2)
+        x_rows = x_scales[0].bitcast(I32)
+        for j, part in enumerate((0, 1, 16, 17)):
+            nc.sync.dma_start(run_bytes[:].bitcast(I32)[part:P:32, :], x_rows[j:16:4, :])
+        for i, words in ((2, w3_words), (1, w2_words)):
+            nc.sync.dma_start(raw_w[i][:].bitcast(I32), words[0].bitcast(I32))
+        load_scale_rows(nc.sync, raw_s[2][:], w3_scales)
+        load_scale_rows(nc.sync, raw_s[1][:], w2_scales)
+        n3_t = load_list("n3_t", n3)
+        n4_t = load_list("n4_t", n4)
+
+        w_codes = [sb.tile([P, 2 * N], U8, name=f"w_codes{i}", align_bytes=64) for i in range(3)]
+        w_scal = [sb.tile([P, N], U8, name=f"w_scal{i}", align_bytes=64) for i in range(3)]
+        xq_scales = sb.tile([P, S], U8, name="xq_scales", align_bytes=64)
+        xq_codes = sb.tile([P, S], U32, name="xq_codes", align_bytes=64)
+        nc.vector.tensor_copy(xq_scales[:], x_bytes[:].indirect(offs_t[:]))
+        deal_words(w_codes[0][:], raw_w[0][:])
+        nc.vector.tensor_copy(xq_codes[:], x_codes[:].indirect(offs_t[:]))
+        deal_scales(w_scal[0][:], raw_s[0][:])
+
+        def product(bank, i, t, codes, scales, start, stop):
+            nc.tensor.matmul_mx(
+                out=bank[:],
+                lhsT=w_codes[i][:, 2 * P * t : 2 * P * (t + 1)].bitcast(FP4X4),
+                lhsT_scale=w_scal[i][:, P * t : P * (t + 1)],
+                rhs=codes[:].bitcast(FP8X4),
+                rhs_scale=scales[:],
+                start=start,
+                stop=stop,
+            )
+
+        y_banks = [psum.tile([P, S], F32, name=f"y_bank{t}") for t in range(PACK)]
+        for t in range(PACK):
+            product(y_banks[t], 0, t, xq_codes, xq_scales, True, True)
+
+        hz_bytes = sb.tile([P, S], U8, name="hz_bytes", align_bytes=64)
+        hz_codes = sb.tile([P, S], U32, name="hz_codes", tag="raw_s0", align_bytes=64)
+        nc.vector.tensor_copy(hz_codes[:], x_codes[:].indirect(hz_t[:]))
+        nc.vector.tensor_copy(hz_bytes[:], run_bytes[:].indirect(hz_t[:]))
+        for dst, src in ((0, 0), (1, 1), (2, 16), (3, 17)):
+            nc.sync.dma_start(hz_scales[:].bitcast(I32)[dst:P:32, :], hz_bytes[:].bitcast(I32)[src:P:32, :])
+        for i in (2, 1):
+            deal_words(w_codes[i][:], raw_w[i][:])
+            deal_scales(w_scal[i][:], raw_s[i][:])
+        h_banks = [psum.tile([P, S], F32, name=f"h_bank{t}") for t in range(PACK)]
+        for t in range(PACK):
+            product(h_banks[t], 2, t, hz_codes, hz_scales, True, False)
+
+        z_tiles = []
+        for t in range(PACK):
+            y = sb.tile([P, S], F32, name=f"y{t}", tag=f"y{t}", align_bytes=64)
+            nc.scalar.activation(y[:], y_banks[t][:], ACT.Copy, scale=gain[:, t : t + 1])
+            pa = sb.tile([P, W], F32, name=f"pa{t}")
+            nb = sb.tile([P, W], F32, name=f"nb{t}")
+            pa75 = sb.tile([P, W], F32, name=f"pa75{t}")
+            pb75 = sb.tile([P, W], F32, name=f"pb75{t}")
+            nc.scalar.activation(pa[:], y[:].indirect(n1_t[:]), ACT.Copy)
+            nc.scalar.activation(nb[:], y[:].indirect(n2_t[:]), ACT.Copy, scale=-1.0)
+            nc.scalar.activation(pa75[:], pa[:], ACT.Copy, scale=0.75)
+            nc.scalar.activation(pb75[:], nb[:], ACT.Copy, scale=-0.75)
+            z = sb.tile([P, S], F32, name=f"z{t}")
+            nc.vector.tensor_tensor(z[:].indirect(n2_t[:]), pa[:], nb[:], ALU.add)
+            nc.vector.tensor_tensor(z[:].indirect(n1_t[:]), pa75[:], pb75[:], ALU.add)
+            z_tiles.append(z)
+        z_planes = sb.tile([P, PACK, S], BF16, name="z_planes", tag=f"y{PACK - 1}", align_bytes=64)
+        for t in range(PACK - 1):
+            nc.scalar.copy(z_planes[:, t, :], z_tiles[t][:])
+        nc.vector.tensor_copy(z_planes[:, PACK - 1, :], z_tiles[PACK - 1][:])
+        z_grouped = sb.tile([P, S, PACK], BF16, name="z_grouped", align_bytes=64)
+        interleave(nc.vector.tensor_copy, z_grouped, z_planes, 0, 352)
+        interleave(nc.scalar.copy, z_grouped, z_planes, 352, S)
+        z_codes = sb.tile([P, S], U32, name="z_codes", align_bytes=64)
+        z_scales = sb.tile([P, S], U8, name="z_scales", align_bytes=64)
+        nc.vector.quantize_mx(
+            out=z_codes[:].bitcast(FP8X4), scales=z_scales[:], in_=z_grouped[:].rearrange("p c t -> p (c t)")
+        )
+        for t in range(PACK):
+            product(h_banks[t], 1, t, z_codes, z_scales, False, True)
+
+        out_rows = out_0.rearrange("(p t) c -> p t c", t=PACK)
+        h_tiles = [sb.tile([P, S], F32, name=f"h{t}") for t in range(PACK)]
+        for t in range(PACK):
+            h = h_tiles[t]
+            if t % 2 == 0:
+                nc.scalar.copy(h[:], h_banks[t][:])
+            else:
+                nc.vector.tensor_copy(h[:], h_banks[t][:])
+            pa2 = sb.tile([P, G], F32, name=f"pa2{t}")
+            size = sb.tile([P, G], F32, name=f"size{t}")
+            root = sb.tile([P, G], F32, name=f"root{t}", tag=f"root{t}", align_bytes=64)
+            old = sb.tile([P, G], F32, name=f"old{t}")
+            if t == 1:
+                nc.vector.tensor_copy(pa2[:], h[:].indirect(n4_t[:]))
+            else:
+                nc.scalar.activation(pa2[:], h[:].indirect(n4_t[:]), ACT.Copy)
+            nc.scalar.activation(size[:], pa2[:], ACT.Abs)
+            nc.scalar.activation(root[:], size[:], ACT.Abs_reciprocal_sqrt, bias=half[:])
+            if t == 2:
+                factor = root
+                nc.vector.tensor_tensor(old[:], h[:].indirect(n3_t[:]), root[:], ALU.mult)
+            else:
+                factor = sb.tile([P, G], F32, name=f"recip{t}")
+                nc.scalar.activation(factor[:], root[:], ACT.Square)
+                if t == 0:
+                    nc.vector.tensor_copy(old[:], h[:].indirect(n3_t[:]))
+                else:
+                    nc.scalar.activation(old[:], h[:].indirect(n3_t[:]), ACT.Copy)
+            nc.vector.tensor_tensor(h[:].indirect(n3_t[:]), old[:], factor[:], ALU.mult)
+            nc.sync.dma_start(out_rows[:, t, :], h[:])
+        o_planes = sb.tile([P, PACK, S], BF16, name="o_planes", tag=f"root{PACK - 1}", align_bytes=64)
+        for t in range(PACK - 1):
+            nc.scalar.copy(o_planes[:, t, :], h_tiles[t][:])
+        nc.vector.tensor_copy(o_planes[:, PACK - 1, :], h_tiles[PACK - 1][:])
+        o_grouped = sb.tile([P, S, PACK], BF16, name="o_grouped", align_bytes=64)
+        interleave(nc.vector.tensor_copy, o_grouped, o_planes, 0, 352)
+        interleave(nc.scalar.copy, o_grouped, o_planes, 352, S)
+        o_codes = sb.tile([P, S], U32, name="o_codes", align_bytes=64)
+        o_scales = sb.tile([P, S], U8, name="o_scales", align_bytes=64)
+        nc.vector.quantize_mx(
+            out=o_codes[:].bitcast(FP8X4), scales=o_scales[:], in_=o_grouped[:].rearrange("p c t -> p (c t)")
+        )
+        nc.sync.dma_start(out_1[0].rearrange("p c r -> p (c r)").bitcast(I32), o_codes[:].bitcast(I32))
+        out_scale_rows = out_2[0].bitcast(I32)
+        for q in range(4):
+            nc.scalar.dma_start(out_scale_rows[4 * q : 4 * q + 4, :], o_scales[:].bitcast(I32)[32 * q : 32 * q + 4, :])

@@ -18,6 +18,7 @@ ALU = mybir.AluOpType
 
 P = 128
 PACK = 4
+SPLIT = 352
 
 
 def tile_picked_mixhhaarknorm_none_po_kernel(
@@ -28,6 +29,7 @@ def tile_picked_mixhhaarknorm_none_po_kernel(
     with ExitStack() as ctx:
         lists = ctx.enter_context(tc.tile_pool(name="lists", bufs=1))
         sb = ctx.enter_context(tc.tile_pool(name="sb", bufs=1))
+        stair = ctx.enter_context(tc.tile_pool(name="stair", bufs=1))
         psum = ctx.enter_context(tc.psum_pool(name="psum", bufs=1))
 
         def load_list(name, dram):
@@ -71,6 +73,8 @@ def tile_picked_mixhhaarknorm_none_po_kernel(
         half = sb.tile([P, 1], F32, name="half")
         nc.gpsimd.memset(half[:], 0.5)
 
+        warm = sb.tile([P, 1], F32, name="warm")
+        nc.scalar.activation(warm[:], half[:], ACT.Abs_reciprocal_sqrt, bias=half[:])
         load_scale_rows(nc.sync, x_bytes[:], x_scales)
         offs_t = load_list("offs_t", offs)
         raw_w = [sb.tile([P, 2 * N], U8, name=f"raw_w{i}", align_bytes=64) for i in range(3)]
@@ -79,15 +83,15 @@ def tile_picked_mixhhaarknorm_none_po_kernel(
         x_codes = sb.tile([P, T], U32, name="x_codes", align_bytes=64)
         nc.sync.dma_start(x_codes[:].bitcast(I32), x_words[0].rearrange("p c r -> p (c r)").bitcast(I32))
         load_scale_rows(nc.sync, raw_s[0][:], w1_scales)
-        gain = sb.tile([P, PACK], F32, name="gain")
-        nc.sync.dma_start(gain[:], gn.rearrange("(p t) o -> p (t o)", t=PACK))
-        n1_t = load_list("n1_t", n1)
-        n2_t = load_list("n2_t", n2)
         x_rows = x_scales[0].bitcast(I32)
         for j, part in enumerate((0, 1, 16, 17)):
             nc.sync.dma_start(run_bytes[:].bitcast(I32)[part:P:32, :], x_rows[j:16:4, :])
+        gain = sb.tile([P, PACK], F32, name="gain")
+        nc.sync.dma_start(gain[:], gn.rearrange("(p t) o -> p (t o)", t=PACK))
         for i, words in ((2, w3_words), (1, w2_words)):
             nc.sync.dma_start(raw_w[i][:].bitcast(I32), words[0].bitcast(I32))
+        n1_t = load_list("n1_t", n1)
+        n2_t = load_list("n2_t", n2)
         load_scale_rows(nc.sync, raw_s[2][:], w3_scales)
         load_scale_rows(nc.sync, raw_s[1][:], w2_scales)
         n3_t = load_list("n3_t", n3)
@@ -104,18 +108,18 @@ def tile_picked_mixhhaarknorm_none_po_kernel(
 
         def product(bank, i, t, codes, scales, start, stop):
             nc.tensor.matmul_mx(
-                out=bank[:],
+                out=bank,
                 lhsT=w_codes[i][:, 2 * P * t : 2 * P * (t + 1)].bitcast(FP4X4),
                 lhsT_scale=w_scal[i][:, P * t : P * (t + 1)],
-                rhs=codes[:].bitcast(FP8X4),
-                rhs_scale=scales[:],
+                rhs=codes.bitcast(FP8X4),
+                rhs_scale=scales,
                 start=start,
                 stop=stop,
             )
 
-        y_banks = [psum.tile([P, S], F32, name=f"y_bank{t}") for t in range(PACK)]
+        y_banks = [psum.tile([P, S], F32, name=f"y_bank{t}", tag=f"y_bank{t}") for t in range(PACK)]
         for t in range(PACK):
-            product(y_banks[t], 0, t, xq_codes, xq_scales, True, True)
+            product(y_banks[t][:], 0, t, xq_codes[:], xq_scales[:], True, True)
 
         hz_bytes = sb.tile([P, S], U8, name="hz_bytes", align_bytes=64)
         hz_codes = sb.tile([P, S], U32, name="hz_codes", tag="raw_s0", align_bytes=64)
@@ -126,84 +130,119 @@ def tile_picked_mixhhaarknorm_none_po_kernel(
         for i in (2, 1):
             deal_words(w_codes[i][:], raw_w[i][:])
             deal_scales(w_scal[i][:], raw_s[i][:])
-        h_banks = [psum.tile([P, S], F32, name=f"h_bank{t}") for t in range(PACK)]
-        for t in range(PACK):
-            product(h_banks[t], 2, t, hz_codes, hz_scales, True, False)
 
-        z_tiles = []
-        for t in range(PACK):
-            y = sb.tile([P, S], F32, name=f"y{t}", tag=f"y{t}", align_bytes=64)
+        z_tiles = [sb.tile([P, S], F32, name=f"z{t}") for t in range(PACK)]
+        pas = [sb.tile([P, W], F32, name=f"pa{t}") for t in range(PACK)]
+        nbs = [sb.tile([P, W], F32, name=f"nb{t}") for t in range(PACK)]
+
+        def differences(t):
+            y = stair.tile([P, S], F32, name=f"y{t}", offset=4 * W * t)
             nc.scalar.activation(y[:], y_banks[t][:], ACT.Copy, scale=gain[:, t : t + 1])
-            pa = sb.tile([P, W], F32, name=f"pa{t}")
-            nb = sb.tile([P, W], F32, name=f"nb{t}")
-            pa75 = sb.tile([P, W], F32, name=f"pa75{t}")
+            nc.scalar.activation(pas[t][:], y[:].indirect(n1_t[:]), ACT.Copy)
+            nc.scalar.activation(nbs[t][:], y[:].indirect(n2_t[:]), ACT.Copy, scale=-1.0)
+            nc.vector.tensor_tensor(z_tiles[t][:].indirect(n2_t[:]), pas[t][:], nbs[t][:], ALU.add)
+
+        def sums(t):
+            if t < PACK - 1:
+                pa75 = stair.tile([P, W], F32, name=f"pa75{t}", offset=4 * W * (t + 1))
+            else:
+                pa75 = sb.tile([P, W], F32, name=f"pa75{t}")
             pb75 = sb.tile([P, W], F32, name=f"pb75{t}")
-            nc.scalar.activation(pa[:], y[:].indirect(n1_t[:]), ACT.Copy)
-            nc.scalar.activation(nb[:], y[:].indirect(n2_t[:]), ACT.Copy, scale=-1.0)
-            nc.scalar.activation(pa75[:], pa[:], ACT.Copy, scale=0.75)
-            nc.scalar.activation(pb75[:], nb[:], ACT.Copy, scale=-0.75)
-            z = sb.tile([P, S], F32, name=f"z{t}")
-            nc.vector.tensor_tensor(z[:].indirect(n2_t[:]), pa[:], nb[:], ALU.add)
-            nc.vector.tensor_tensor(z[:].indirect(n1_t[:]), pa75[:], pb75[:], ALU.add)
-            z_tiles.append(z)
-        z_planes = sb.tile([P, PACK, S], BF16, name="z_planes", tag=f"y{PACK - 1}", align_bytes=64)
+            nc.scalar.activation(pa75[:], pas[t][:], ACT.Copy, scale=0.75)
+            nc.scalar.activation(pb75[:], nbs[t][:], ACT.Copy, scale=-0.75)
+            nc.vector.tensor_tensor(z_tiles[t][:].indirect(n1_t[:]), pa75[:], pb75[:], ALU.add)
+
+        differences(0)
+        for t in range(1, PACK):
+            differences(t)
+            sums(t - 1)
+        sums(PACK - 1)
+
+        halves = (slice(0, S // 2), slice(S // 2, S))
+        h0_banks = [
+            psum.tile([P, S // 2], F32, name="h0_left"),
+            psum.tile([P, S // 2], F32, name="h0_right", tag="y_bank0"),
+        ]
+        h_banks = [None] + [psum.tile([P, S], F32, name=f"h_bank{t}") for t in range(1, PACK)]
+        for bank, cols in zip(h0_banks, halves):
+            product(bank[:], 2, 0, hz_codes[:, cols], hz_scales[:, cols], True, False)
+        for t in range(1, PACK):
+            product(h_banks[t][:], 2, t, hz_codes[:], hz_scales[:], True, False)
+
+        def quantise(planes, name):
+            grouped = sb.tile([P, S, PACK], BF16, name=f"{name}_grouped", align_bytes=64)
+            codes = sb.tile([P, S], U32, name=f"{name}_codes", align_bytes=64)
+            scales = sb.tile([P, S], U8, name=f"{name}_scales", align_bytes=64)
+            interleave(nc.vector.tensor_copy, grouped, planes, 0, S // 2)
+            interleave(nc.scalar.copy, grouped, planes, SPLIT, S)
+            interleave(nc.vector.tensor_copy, grouped, planes, S // 2, SPLIT)
+            for cols in halves:
+                nc.vector.quantize_mx(
+                    out=codes[:, cols].bitcast(FP8X4),
+                    scales=scales[:, cols],
+                    in_=grouped[:, cols, :].rearrange("p c t -> p (c t)"),
+                )
+            return codes, scales
+
+        z_planes = stair.tile([P, PACK, S], BF16, name="z_planes", offset=4 * W * PACK, align_bytes=64)
         for t in range(PACK - 1):
             nc.scalar.copy(z_planes[:, t, :], z_tiles[t][:])
-        nc.vector.tensor_copy(z_planes[:, PACK - 1, :], z_tiles[PACK - 1][:])
-        z_grouped = sb.tile([P, S, PACK], BF16, name="z_grouped", align_bytes=64)
-        interleave(nc.vector.tensor_copy, z_grouped, z_planes, 0, 352)
-        interleave(nc.scalar.copy, z_grouped, z_planes, 352, S)
-        z_codes = sb.tile([P, S], U32, name="z_codes", align_bytes=64)
-        z_scales = sb.tile([P, S], U8, name="z_scales", align_bytes=64)
-        nc.vector.quantize_mx(
-            out=z_codes[:].bitcast(FP8X4), scales=z_scales[:], in_=z_grouped[:].rearrange("p c t -> p (c t)")
-        )
-        for t in range(PACK):
-            product(h_banks[t], 1, t, z_codes, z_scales, False, True)
+        last = PACK - 1
+        nc.vector.tensor_copy(z_planes[:, last, 0 : S // 2], z_tiles[last][:, 0 : S // 2])
+        nc.scalar.copy(z_planes[:, last, SPLIT:S], z_tiles[last][:, SPLIT:S])
+        nc.vector.tensor_copy(z_planes[:, last, S // 2 : SPLIT], z_tiles[last][:, S // 2 : SPLIT])
+        z_codes, z_scales = quantise(z_planes, "z")
+        for bank, cols in zip(h0_banks, halves):
+            product(bank[:], 1, 0, z_codes[:, cols], z_scales[:, cols], False, True)
+        for t in range(1, PACK):
+            product(h_banks[t][:], 1, t, z_codes[:], z_scales[:], False, True)
 
         out_rows = out_0.rearrange("(p t) c -> p t c", t=PACK)
         h_tiles = [sb.tile([P, S], F32, name=f"h{t}") for t in range(PACK)]
+        roots, parts = [], []
         for t in range(PACK):
             h = h_tiles[t]
-            if t % 2 == 0:
-                nc.scalar.copy(h[:], h_banks[t][:])
+            h_abs = sb.tile([P, S], F32, name=f"h_abs{t}", tag="h_abs", align_bytes=64)
+            if t == 0:
+                for bank, cols in zip(h0_banks, halves):
+                    nc.scalar.activation(h_abs[:, cols], bank[:], ACT.Abs)
+                    nc.vector.tensor_copy(h[:, cols], bank[:])
             else:
                 nc.vector.tensor_copy(h[:], h_banks[t][:])
-            pa2 = sb.tile([P, G], F32, name=f"pa2{t}")
-            size = sb.tile([P, G], F32, name=f"size{t}")
-            root = sb.tile([P, G], F32, name=f"root{t}", tag=f"root{t}", align_bytes=64)
-            old = sb.tile([P, G], F32, name=f"old{t}")
-            if t == 1:
-                nc.vector.tensor_copy(pa2[:], h[:].indirect(n4_t[:]))
-            else:
-                nc.scalar.activation(pa2[:], h[:].indirect(n4_t[:]), ACT.Copy)
-            nc.scalar.activation(size[:], pa2[:], ACT.Abs)
+                nc.scalar.activation(h_abs[:], h_banks[t][:], ACT.Abs)
+            size = sb.tile([P, G], F32, name=f"size{t}", tag=f"size{t}")
+            root = sb.tile([P, G], F32, name=f"root{t}")
+            nc.scalar.activation(size[:], h_abs[:].indirect(n4_t[:]), ACT.Copy)
             nc.scalar.activation(root[:], size[:], ACT.Abs_reciprocal_sqrt, bias=half[:])
-            if t == 2:
-                factor = root
-                nc.vector.tensor_tensor(old[:], h[:].indirect(n3_t[:]), root[:], ALU.mult)
-            else:
-                factor = sb.tile([P, G], F32, name=f"recip{t}")
+            if t == 1:
+                part = sb.tile([P, G], F32, name="part1", tag="size0")
+                factor = sb.tile([P, G], F32, name="recip")
                 nc.scalar.activation(factor[:], root[:], ACT.Square)
-                if t == 0:
-                    nc.vector.tensor_copy(old[:], h[:].indirect(n3_t[:]))
-                else:
-                    nc.scalar.activation(old[:], h[:].indirect(n3_t[:]), ACT.Copy)
-            nc.vector.tensor_tensor(h[:].indirect(n3_t[:]), old[:], factor[:], ALU.mult)
-            nc.sync.dma_start(out_rows[:, t, :], h[:])
-        o_planes = sb.tile([P, PACK, S], BF16, name="o_planes", tag=f"root{PACK - 1}", align_bytes=64)
-        for t in range(PACK - 1):
+                nc.scalar.activation(part[:], h[:].indirect(n3_t[:]), ACT.Copy)
+            else:
+                part = sb.tile([P, G], F32, name=f"part{t}")
+                factor = root
+            if t == 3:
+                ra2 = sb.tile([P, G], F32, name="ra2", tag="size3")
+                nc.vector.tensor_tensor(ra2[:], parts[2][:], roots[2][:], ALU.mult)
+            if t != 1:
+                nc.vector.tensor_tensor(part[:], h[:].indirect(n3_t[:]), root[:], ALU.mult)
+            if t != 2:
+                nc.vector.tensor_tensor(h[:].indirect(n3_t[:]), part[:], factor[:], ALU.mult)
+                nc.sync.dma_start(out_rows[:, t, :], h[:])
+            roots.append(root)
+            parts.append(part)
+        o_planes = sb.tile([P, PACK, S], BF16, name="o_planes", tag="h_abs", align_bytes=64)
+        for t in range(2):
             nc.scalar.copy(o_planes[:, t, :], h_tiles[t][:])
+        nc.scalar.activation(h_tiles[2][:].indirect(n3_t[:]), ra2[:], ACT.Copy)
+        nc.sync.dma_start(out_rows[:, 2, :], h_tiles[2][:])
+        nc.scalar.copy(o_planes[:, 2, :], h_tiles[2][:])
         nc.vector.tensor_copy(o_planes[:, PACK - 1, :], h_tiles[PACK - 1][:])
-        o_grouped = sb.tile([P, S, PACK], BF16, name="o_grouped", align_bytes=64)
-        interleave(nc.vector.tensor_copy, o_grouped, o_planes, 0, 352)
-        interleave(nc.scalar.copy, o_grouped, o_planes, 352, S)
-        o_codes = sb.tile([P, S], U32, name="o_codes", align_bytes=64)
-        o_scales = sb.tile([P, S], U8, name="o_scales", align_bytes=64)
-        nc.vector.quantize_mx(
-            out=o_codes[:].bitcast(FP8X4), scales=o_scales[:], in_=o_grouped[:].rearrange("p c t -> p (c t)")
-        )
-        nc.sync.dma_start(out_1[0].rearrange("p c r -> p (c r)").bitcast(I32), o_codes[:].bitcast(I32))
+        o_codes, o_scales = quantise(o_planes, "o")
+        out_words = out_1[0].rearrange("p c r -> p (c r)").bitcast(I32)
+        for cols in halves:
+            nc.sync.dma_start(out_words[:, cols], o_codes[:, cols].bitcast(I32))
         out_scale_rows = out_2[0].bitcast(I32)
         for q in range(4):
             nc.scalar.dma_start(out_scale_rows[4 * q : 4 * q + 4, :], o_scales[:].bitcast(I32)[32 * q : 32 * q + 4, :])

@@ -30,6 +30,7 @@ def tile_picked_mixhhaarknorm_none_po_kernel(
         lists = ctx.enter_context(tc.tile_pool(name="lists", bufs=1))
         sb = ctx.enter_context(tc.tile_pool(name="sb", bufs=1))
         stair = ctx.enter_context(tc.tile_pool(name="stair", bufs=1))
+        head = ctx.enter_context(tc.tile_pool(name="head", bufs=1))
         psum = ctx.enter_context(tc.psum_pool(name="psum", bufs=1))
 
         def load_list(name, dram):
@@ -62,7 +63,8 @@ def tile_picked_mixhhaarknorm_none_po_kernel(
 
         x_bytes = sb.tile([P, T], U8, name="x_bytes", align_bytes=64)
         nc.vector.memset(x_bytes[:].bitcast(I32), 0)
-        raw_s = [sb.tile([P, N], U8, name=f"raw_s{i}", tag=f"raw_s{i}", align_bytes=64) for i in range(3)]
+        raw_s = [head.tile([P, N], U8, name="raw_s0", offset=768, align_bytes=64)]
+        raw_s = raw_s + [sb.tile([P, N], U8, name=f"raw_s{i}", align_bytes=64) for i in (1, 2)]
         nc.vector.memset(raw_s[0][:].bitcast(I32), 0)
         run_bytes = sb.tile([P, T], U8, name="run_bytes", align_bytes=64)
         nc.gpsimd.memset(run_bytes[:].bitcast(I32), 0)
@@ -83,11 +85,11 @@ def tile_picked_mixhhaarknorm_none_po_kernel(
         x_codes = sb.tile([P, T], U32, name="x_codes", align_bytes=64)
         nc.sync.dma_start(x_codes[:].bitcast(I32), x_words[0].rearrange("p c r -> p (c r)").bitcast(I32))
         load_scale_rows(nc.sync, raw_s[0][:], w1_scales)
+        gain = sb.tile([P, PACK], F32, name="gain")
+        nc.sync.dma_start(gain[:], gn.rearrange("(p t) o -> p (t o)", t=PACK))
         x_rows = x_scales[0].bitcast(I32)
         for j, part in enumerate((0, 1, 16, 17)):
             nc.sync.dma_start(run_bytes[:].bitcast(I32)[part:P:32, :], x_rows[j:16:4, :])
-        gain = sb.tile([P, PACK], F32, name="gain")
-        nc.sync.dma_start(gain[:], gn.rearrange("(p t) o -> p (t o)", t=PACK))
         for i, words in ((2, w3_words), (1, w2_words)):
             nc.sync.dma_start(raw_w[i][:].bitcast(I32), words[0].bitcast(I32))
         n1_t = load_list("n1_t", n1)
@@ -100,11 +102,14 @@ def tile_picked_mixhhaarknorm_none_po_kernel(
         w_codes = [sb.tile([P, 2 * N], U8, name=f"w_codes{i}", align_bytes=64) for i in range(3)]
         w_scal = [sb.tile([P, N], U8, name=f"w_scal{i}", align_bytes=64) for i in range(3)]
         xq_scales = sb.tile([P, S], U8, name="xq_scales", align_bytes=64)
-        xq_codes = sb.tile([P, S], U32, name="xq_codes", align_bytes=64)
+        halves = (slice(0, S // 2), slice(S // 2, S))
+        xq_left = sb.tile([P, S // 2], U32, name="xq_left", align_bytes=64)
+        xq_right = head.tile([P, S // 2], U32, name="xq_right", offset=0, align_bytes=64)
         nc.vector.tensor_copy(xq_scales[:], x_bytes[:].indirect(offs_t[:]))
         deal_words(w_codes[0][:], raw_w[0][:])
-        nc.vector.tensor_copy(xq_codes[:], x_codes[:].indirect(offs_t[:]))
+        nc.vector.tensor_copy(xq_left[:], x_codes[:].indirect(offs_t[:, 0:16]))
         deal_scales(w_scal[0][:], raw_s[0][:])
+        nc.vector.tensor_copy(xq_right[:], x_codes[:].indirect(offs_t[:, 16:32]))
 
         def product(bank, i, t, codes, scales, start, stop):
             nc.tensor.matmul_mx(
@@ -117,12 +122,19 @@ def tile_picked_mixhhaarknorm_none_po_kernel(
                 stop=stop,
             )
 
-        y_banks = [psum.tile([P, S], F32, name=f"y_bank{t}", tag=f"y_bank{t}") for t in range(PACK)]
-        for t in range(PACK):
-            product(y_banks[t][:], 0, t, xq_codes[:], xq_scales[:], True, True)
+        y0_banks = [
+            psum.tile([P, S // 2], F32, name="y0_left", tag="bank_a"),
+            psum.tile([P, S // 2], F32, name="y0_right", tag="bank_b"),
+        ]
+        y_banks = [None] + [psum.tile([P, S], F32, name=f"y_bank{t}") for t in range(1, PACK)]
+        for bank, codes, cols in zip(y0_banks, (xq_left, xq_right), halves):
+            product(bank[:], 0, 0, codes[:], xq_scales[:, cols], True, True)
+        for t in range(1, PACK):
+            product(y_banks[t][:, halves[1]], 0, t, xq_right[:], xq_scales[:, halves[1]], True, True)
+            product(y_banks[t][:, halves[0]], 0, t, xq_left[:], xq_scales[:, halves[0]], True, True)
 
         hz_bytes = sb.tile([P, S], U8, name="hz_bytes", align_bytes=64)
-        hz_codes = sb.tile([P, S], U32, name="hz_codes", tag="raw_s0", align_bytes=64)
+        hz_codes = head.tile([P, S], U32, name="hz_codes", offset=1024, align_bytes=64)
         nc.vector.tensor_copy(hz_codes[:], x_codes[:].indirect(hz_t[:]))
         nc.vector.tensor_copy(hz_bytes[:], run_bytes[:].indirect(hz_t[:]))
         for dst, src in ((0, 0), (1, 1), (2, 16), (3, 17)):
@@ -137,7 +149,11 @@ def tile_picked_mixhhaarknorm_none_po_kernel(
 
         def differences(t):
             y = stair.tile([P, S], F32, name=f"y{t}", offset=4 * W * t)
-            nc.scalar.activation(y[:], y_banks[t][:], ACT.Copy, scale=gain[:, t : t + 1])
+            if t == 0:
+                for bank, cols in zip(y0_banks, halves):
+                    nc.scalar.activation(y[:, cols], bank[:], ACT.Copy, scale=gain[:, 0:1])
+            else:
+                nc.scalar.activation(y[:], y_banks[t][:], ACT.Copy, scale=gain[:, t : t + 1])
             nc.scalar.activation(pas[t][:], y[:].indirect(n1_t[:]), ACT.Copy)
             nc.scalar.activation(nbs[t][:], y[:].indirect(n2_t[:]), ACT.Copy, scale=-1.0)
             nc.vector.tensor_tensor(z_tiles[t][:].indirect(n2_t[:]), pas[t][:], nbs[t][:], ALU.add)
@@ -158,10 +174,9 @@ def tile_picked_mixhhaarknorm_none_po_kernel(
             sums(t - 1)
         sums(PACK - 1)
 
-        halves = (slice(0, S // 2), slice(S // 2, S))
         h0_banks = [
-            psum.tile([P, S // 2], F32, name="h0_left"),
-            psum.tile([P, S // 2], F32, name="h0_right", tag="y_bank0"),
+            psum.tile([P, S // 2], F32, name="h0_left", tag="bank_a"),
+            psum.tile([P, S // 2], F32, name="h0_right", tag="bank_b"),
         ]
         h_banks = [None] + [psum.tile([P, S], F32, name=f"h_bank{t}") for t in range(1, PACK)]
         for bank, cols in zip(h0_banks, halves):
@@ -214,21 +229,14 @@ def tile_picked_mixhhaarknorm_none_po_kernel(
             root = sb.tile([P, G], F32, name=f"root{t}")
             nc.scalar.activation(size[:], h_abs[:].indirect(n4_t[:]), ACT.Copy)
             nc.scalar.activation(root[:], size[:], ACT.Abs_reciprocal_sqrt, bias=half[:])
-            if t == 1:
-                part = sb.tile([P, G], F32, name="part1", tag="size0")
-                factor = sb.tile([P, G], F32, name="recip")
-                nc.scalar.activation(factor[:], root[:], ACT.Square)
-                nc.scalar.activation(part[:], h[:].indirect(n3_t[:]), ACT.Copy)
-            else:
-                part = sb.tile([P, G], F32, name=f"part{t}")
-                factor = root
+            part = sb.tile([P, G], F32, name=f"part{t}")
             if t == 3:
                 ra2 = sb.tile([P, G], F32, name="ra2", tag="size3")
                 nc.vector.tensor_tensor(ra2[:], parts[2][:], roots[2][:], ALU.mult)
-            if t != 1:
+            if True:
                 nc.vector.tensor_tensor(part[:], h[:].indirect(n3_t[:]), root[:], ALU.mult)
             if t != 2:
-                nc.vector.tensor_tensor(h[:].indirect(n3_t[:]), part[:], factor[:], ALU.mult)
+                nc.vector.tensor_tensor(h[:].indirect(n3_t[:]), part[:], root[:], ALU.mult)
                 nc.sync.dma_start(out_rows[:, t, :], h[:])
             roots.append(root)
             parts.append(part)

@@ -66,8 +66,6 @@ def tile_picked_mixhhaarknorm_none_po_kernel(
         raw_s = [head.tile([P, N], U8, name="raw_s0", offset=768, align_bytes=64)]
         raw_s = raw_s + [sb.tile([P, N], U8, name=f"raw_s{i}", align_bytes=64) for i in (1, 2)]
         nc.vector.memset(raw_s[0][:].bitcast(I32), 0)
-        run_bytes = sb.tile([P, T], U8, name="run_bytes", align_bytes=64)
-        nc.gpsimd.memset(run_bytes[:].bitcast(I32), 0)
         for i in (2, 1):
             nc.gpsimd.memset(raw_s[i][:].bitcast(I32), 0)
         hz_scales = sb.tile([P, S], U8, name="hz_scales", align_bytes=64)
@@ -77,7 +75,10 @@ def tile_picked_mixhhaarknorm_none_po_kernel(
 
         warm = sb.tile([P, 1], F32, name="warm")
         nc.scalar.activation(warm[:], half[:], ACT.Abs_reciprocal_sqrt, bias=half[:])
-        load_scale_rows(nc.sync, x_bytes[:], x_scales)
+        x_rows = x_scales[0].bitcast(I32)
+        nc.sync.dma_start(x_bytes[:].bitcast(I32)[0:P:8, :], x_rows)
+        for j in range(1, 4):
+            nc.sync.dma_start(x_bytes[:].bitcast(I32)[j:P:32, :], x_rows[j:16:4, :])
         offs_t = load_list("offs_t", offs)
         raw_w = [sb.tile([P, 2 * N], U8, name=f"raw_w{i}", align_bytes=64) for i in range(3)]
         nc.sync.dma_start(raw_w[0][:].bitcast(I32), w1_words[0].bitcast(I32))
@@ -85,17 +86,14 @@ def tile_picked_mixhhaarknorm_none_po_kernel(
         x_codes = sb.tile([P, T], U32, name="x_codes", align_bytes=64)
         nc.sync.dma_start(x_codes[:].bitcast(I32), x_words[0].rearrange("p c r -> p (c r)").bitcast(I32))
         load_scale_rows(nc.sync, raw_s[0][:], w1_scales)
-        gain = sb.tile([P, PACK], F32, name="gain")
-        nc.sync.dma_start(gain[:], gn.rearrange("(p t) o -> p (t o)", t=PACK))
-        x_rows = x_scales[0].bitcast(I32)
-        for j, part in enumerate((0, 1, 16, 17)):
-            nc.sync.dma_start(run_bytes[:].bitcast(I32)[part:P:32, :], x_rows[j:16:4, :])
         for i, words in ((2, w3_words), (1, w2_words)):
             nc.sync.dma_start(raw_w[i][:].bitcast(I32), words[0].bitcast(I32))
+        load_scale_rows(nc.sync, raw_s[2][:], w3_scales)
         n1_t = load_list("n1_t", n1)
         n2_t = load_list("n2_t", n2)
-        load_scale_rows(nc.sync, raw_s[2][:], w3_scales)
         load_scale_rows(nc.sync, raw_s[1][:], w2_scales)
+        gain = sb.tile([P, PACK], F32, name="gain")
+        nc.sync.dma_start(gain[:], gn.rearrange("(p t) o -> p (t o)", t=PACK))
         n3_t = load_list("n3_t", n3)
         n4_t = load_list("n4_t", n4)
 
@@ -106,6 +104,8 @@ def tile_picked_mixhhaarknorm_none_po_kernel(
         xq_left = sb.tile([P, S // 2], U32, name="xq_left", align_bytes=64)
         xq_right = head.tile([P, S // 2], U32, name="xq_right", offset=0, align_bytes=64)
         nc.vector.tensor_copy(xq_scales[:], x_bytes[:].indirect(offs_t[:]))
+        hz_bytes = sb.tile([P, S], U8, name="hz_bytes", align_bytes=64)
+        nc.vector.tensor_copy(hz_bytes[:], x_bytes[:].indirect(hz_t[:]))
         deal_words(w_codes[0][:], raw_w[0][:])
         nc.vector.tensor_copy(xq_left[:], x_codes[:].indirect(offs_t[:, 0:16]))
         deal_scales(w_scal[0][:], raw_s[0][:])
@@ -133,14 +133,13 @@ def tile_picked_mixhhaarknorm_none_po_kernel(
             product(y_banks[t][:, halves[1]], 0, t, xq_right[:], xq_scales[:, halves[1]], True, True)
             product(y_banks[t][:, halves[0]], 0, t, xq_left[:], xq_scales[:, halves[0]], True, True)
 
-        hz_bytes = sb.tile([P, S], U8, name="hz_bytes", align_bytes=64)
         hz_codes = head.tile([P, S], U32, name="hz_codes", offset=1024, align_bytes=64)
         nc.vector.tensor_copy(hz_codes[:], x_codes[:].indirect(hz_t[:]))
-        nc.vector.tensor_copy(hz_bytes[:], run_bytes[:].indirect(hz_t[:]))
-        for dst, src in ((0, 0), (1, 1), (2, 16), (3, 17)):
-            nc.sync.dma_start(hz_scales[:].bitcast(I32)[dst:P:32, :], hz_bytes[:].bitcast(I32)[src:P:32, :])
+        for j in range(4):
+            nc.sync.dma_start(hz_scales[:].bitcast(I32)[j:P:32, :], hz_bytes[:].bitcast(I32)[8 * j : P : 32, :])
         for i in (2, 1):
             deal_words(w_codes[i][:], raw_w[i][:])
+        for i in (2, 1):
             deal_scales(w_scal[i][:], raw_s[i][:])
 
         z_tiles = [sb.tile([P, S], F32, name=f"z{t}") for t in range(PACK)]
@@ -151,9 +150,9 @@ def tile_picked_mixhhaarknorm_none_po_kernel(
             y = stair.tile([P, S], F32, name=f"y{t}", offset=4 * W * t)
             if t == 0:
                 for bank, cols in zip(y0_banks, halves):
-                    nc.scalar.activation(y[:, cols], bank[:], ACT.Copy, scale=gain[:, 0:1])
+                    nc.scalar.copy(y[:, cols], bank[:])
             else:
-                nc.scalar.activation(y[:], y_banks[t][:], ACT.Copy, scale=gain[:, t : t + 1])
+                nc.scalar.copy(y[:], y_banks[t][:])
             nc.scalar.activation(pas[t][:], y[:].indirect(n1_t[:]), ACT.Copy)
             nc.scalar.activation(nbs[t][:], y[:].indirect(n2_t[:]), ACT.Copy, scale=-1.0)
             nc.vector.tensor_tensor(z_tiles[t][:].indirect(n2_t[:]), pas[t][:], nbs[t][:], ALU.add)
@@ -201,11 +200,12 @@ def tile_picked_mixhhaarknorm_none_po_kernel(
 
         z_planes = stair.tile([P, PACK, S], BF16, name="z_planes", offset=4 * W * PACK, align_bytes=64)
         for t in range(PACK - 1):
-            nc.scalar.copy(z_planes[:, t, :], z_tiles[t][:])
+            nc.scalar.activation(z_planes[:, t, :], z_tiles[t][:], ACT.Copy, scale=gain[:, t : t + 1])
         last = PACK - 1
-        nc.vector.tensor_copy(z_planes[:, last, 0 : S // 2], z_tiles[last][:, 0 : S // 2])
-        nc.scalar.copy(z_planes[:, last, SPLIT:S], z_tiles[last][:, SPLIT:S])
-        nc.vector.tensor_copy(z_planes[:, last, S // 2 : SPLIT], z_tiles[last][:, S // 2 : SPLIT])
+        last_gain = gain[:, last : last + 1]
+        nc.vector.tensor_scalar_mul(z_planes[:, last, 0 : S // 2], z_tiles[last][:, 0 : S // 2], last_gain)
+        nc.scalar.activation(z_planes[:, last, SPLIT:S], z_tiles[last][:, SPLIT:S], ACT.Copy, scale=last_gain)
+        nc.vector.tensor_scalar_mul(z_planes[:, last, S // 2 : SPLIT], z_tiles[last][:, S // 2 : SPLIT], last_gain)
         z_codes, z_scales = quantise(z_planes, "z")
         for bank, cols in zip(h0_banks, halves):
             product(bank[:], 1, 0, z_codes[:, cols], z_scales[:, cols], False, True)
@@ -233,8 +233,7 @@ def tile_picked_mixhhaarknorm_none_po_kernel(
             if t == 3:
                 ra2 = sb.tile([P, G], F32, name="ra2", tag="size3")
                 nc.vector.tensor_tensor(ra2[:], parts[2][:], roots[2][:], ALU.mult)
-            if True:
-                nc.vector.tensor_tensor(part[:], h[:].indirect(n3_t[:]), root[:], ALU.mult)
+            nc.vector.tensor_tensor(part[:], h[:].indirect(n3_t[:]), root[:], ALU.mult)
             if t != 2:
                 nc.vector.tensor_tensor(h[:].indirect(n3_t[:]), part[:], root[:], ALU.mult)
                 nc.sync.dma_start(out_rows[:, t, :], h[:])
@@ -253,4 +252,5 @@ def tile_picked_mixhhaarknorm_none_po_kernel(
             nc.sync.dma_start(out_words[:, cols], o_codes[:, cols].bitcast(I32))
         out_scale_rows = out_2[0].bitcast(I32)
         for q in range(4):
-            nc.scalar.dma_start(out_scale_rows[4 * q : 4 * q + 4, :], o_scales[:].bitcast(I32)[32 * q : 32 * q + 4, :])
+            queue = nc.sync if q < 2 else nc.scalar
+            queue.dma_start(out_scale_rows[4 * q : 4 * q + 4, :], o_scales[:].bitcast(I32)[32 * q : 32 * q + 4, :])

from contextlib import ExitStack

import concourse.mybir as mybir

K, T, S, N, H, W, G = 512, 2048, 512, 512, 512, 256, 384
FLOPS = 3 * 2 * 512 * 512 * 512

F32 = mybir.dt.float32
BF16 = mybir.dt.bfloat16
I32 = mybir.dt.int32
U32 = mybir.dt.uint32
U16 = mybir.dt.uint16
U8 = mybir.dt.uint8
FP8X4 = mybir.dt.float8_e4m3fn_x4
FP4X4 = mybir.dt.float4_e2m1fn_x4
ACT = mybir.ActivationFunctionType
ALU = mybir.AluOpType

P = 128
PACK = 4
SPLIT = 352


def tile_picked_mixhhaarknorm_none_po_kernel(
    tc, x_words, x_scales, w1_words, w1_scales, gn, w2_words, w2_scales, w3_words, w3_scales,
    offs, n1, n2, hz, n3, n4, out_0, out_1, out_2,
):
    nc = tc.nc
    with ExitStack() as ctx:
        lists = ctx.enter_context(tc.tile_pool(name="lists", bufs=1))
        sb = ctx.enter_context(tc.tile_pool(name="sb", bufs=1))
        stair = ctx.enter_context(tc.tile_pool(name="stair", bufs=1))
        head = ctx.enter_context(tc.tile_pool(name="head", bufs=1))
        psum = ctx.enter_context(tc.psum_pool(name="psum", bufs=1))

        def load_list(name, dram):
            tile = lists.tile(list(dram.shape), U16, name=name)
            nc.sync.dma_start(tile[:], dram)
            return tile

        def load_scale_rows(queue, plane, dram):
            rows = dram[0].bitcast(I32)
            for j in range(4):
                queue.dma_start(plane.bitcast(I32)[j:P:32, :], rows[j:16:4, :])

        def deal_words(dealt, raw):
            nc.vector.tensor_copy(
                out=dealt.bitcast(U16).rearrange("p (t m) -> p t m", t=PACK),
                in_=raw.bitcast(U16).rearrange("p (m t) -> p t m", t=PACK),
            )

        def deal_scales(dealt, raw):
            nc.vector.tensor_copy(
                out=dealt.rearrange("p (t m) -> p t m", t=PACK),
                in_=raw.rearrange("p (m t) -> p t m", t=PACK),
            )

        def interleave(engine_copy, grouped, planes, c0, c1):
            engine_copy(
                out=grouped[:, c0:c1, :].rearrange("p (c i) t -> p c t i", i=4),
                in_=planes[:, :, c0:c1].rearrange("p t (c i) -> p c t i", i=4),
            )

        x_bytes = sb.tile([P, T], U8, name="x_bytes", align_bytes=64)
        nc.vector.memset(x_bytes[:].bitcast(I32), 0)
        raw_s = [head.tile([P, N], U8, name="raw_s0", offset=768, align_bytes=64)]
        raw_s = raw_s + [sb.tile([P, N], U8, name=f"raw_s{i}", align_bytes=64) for i in (1, 2)]
        nc.vector.memset(raw_s[0][:].bitcast(I32), 0)
        for i in (2, 1):
            nc.gpsimd.memset(raw_s[i][:].bitcast(I32), 0)
        hz_scales = sb.tile([P, S], U8, name="hz_scales", align_bytes=64)
        nc.gpsimd.memset(hz_scales[:].bitcast(I32), 0)
        half = sb.tile([P, 1], F32, name="half")
        nc.gpsimd.memset(half[:], 0.5)

        warm = sb.tile([P, 1], F32, name="warm")
        nc.scalar.activation(warm[:], half[:], ACT.Abs_reciprocal_sqrt, bias=half[:])
        x_rows = x_scales[0].bitcast(I32)
        nc.sync.dma_start(x_bytes[:].bitcast(I32)[0:P:8, :], x_rows)
        for j in range(1, 4):
            nc.sync.dma_start(x_bytes[:].bitcast(I32)[j:P:32, :], x_rows[j:16:4, :])
        offs_t = load_list("offs_t", offs)
        raw_w = [sb.tile([P, 2 * N], U8, name=f"raw_w{i}", align_bytes=64) for i in range(3)]
        nc.sync.dma_start(raw_w[0][:].bitcast(I32), w1_words[0].bitcast(I32))
        hz_t = load_list("hz_t", hz)
        x_codes = sb.tile([P, T], U32, name="x_codes", align_bytes=64)
        nc.sync.dma_start(x_codes[:].bitcast(I32), x_words[0].rearrange("p c r -> p (c r)").bitcast(I32))
        load_scale_rows(nc.sync, raw_s[0][:], w1_scales)
        for i, words in ((2, w3_words), (1, w2_words)):
            nc.sync.dma_start(raw_w[i][:].bitcast(I32), words[0].bitcast(I32))
        load_scale_rows(nc.sync, raw_s[2][:], w3_scales)
        n1_t = load_list("n1_t", n1)
        n2_t = load_list("n2_t", n2)
        load_scale_rows(nc.sync, raw_s[1][:], w2_scales)
        gain = sb.tile([P, PACK], F32, name="gain")
        nc.sync.dma_start(gain[:], gn.rearrange("(p t) o -> p (t o)", t=PACK))
        n3_t = load_list("n3_t", n3)
        n4_t = load_list("n4_t", n4)

        w_codes = [sb.tile([P, 2 * N], U8, name=f"w_codes{i}", align_bytes=64) for i in range(3)]
        w_scal = [sb.tile([P, N], U8, name=f"w_scal{i}", align_bytes=64) for i in range(3)]
        xq_scales = sb.tile([P, S], U8, name="xq_scales", align_bytes=64)
        halves = (slice(0, S // 2), slice(S // 2, S))
        xq_left = sb.tile([P, S // 2], U32, name="xq_left", align_bytes=64)
        xq_right = head.tile([P, S // 2], U32, name="xq_right", offset=0, align_bytes=64)
        nc.vector.tensor_copy(xq_scales[:], x_bytes[:].indirect(offs_t[:]))
        hz_bytes = sb.tile([P, S], U8, name="hz_bytes", align_bytes=64)
        nc.vector.tensor_copy(hz_bytes[:], x_bytes[:].indirect(hz_t[:]))
        deal_words(w_codes[0][:], raw_w[0][:])
        nc.vector.tensor_copy(xq_left[:], x_codes[:].indirect(offs_t[:, 0:16]))
        deal_scales(w_scal[0][:], raw_s[0][:])
        nc.vector.tensor_copy(xq_right[:], x_codes[:].indirect(offs_t[:, 16:32]))

        def product(bank, i, t, codes, scales, start, stop):
            nc.tensor.matmul_mx(
                out=bank,
                lhsT=w_codes[i][:, 2 * P * t : 2 * P * (t + 1)].bitcast(FP4X4),
                lhsT_scale=w_scal[i][:, P * t : P * (t + 1)],
                rhs=codes.bitcast(FP8X4),
                rhs_scale=scales,
                start=start,
                stop=stop,
            )

        y0_banks = [
            psum.tile([P, S // 2], F32, name="y0_left", tag="bank_a"),
            psum.tile([P, S // 2], F32, name="y0_right", tag="bank_b"),
        ]
        y_banks = [None] + [psum.tile([P, S], F32, name=f"y_bank{t}") for t in range(1, PACK)]
        for bank, codes, cols in zip(y0_banks, (xq_left, xq_right), halves):
            product(bank[:], 0, 0, codes[:], xq_scales[:, cols], True, True)
        for t in range(1, PACK):
            product(y_banks[t][:, halves[1]], 0, t, xq_right[:], xq_scales[:, halves[1]], True, True)
            product(y_banks[t][:, halves[0]], 0, t, xq_left[:], xq_scales[:, halves[0]], True, True)

        hz_codes = head.tile([P, S], U32, name="hz_codes", offset=1024, align_bytes=64)
        nc.vector.tensor_copy(hz_codes[:], x_codes[:].indirect(hz_t[:]))
        for j in range(4):
            nc.sync.dma_start(hz_scales[:].bitcast(I32)[j:P:32, :], hz_bytes[:].bitcast(I32)[8 * j : P : 32, :])
        for i in (2, 1):
            deal_words(w_codes[i][:], raw_w[i][:])
        for i in (2, 1):
            deal_scales(w_scal[i][:], raw_s[i][:])

        z_tiles = [sb.tile([P, S], F32, name=f"z{t}") for t in range(PACK)]
        pas = [sb.tile([P, W], F32, name=f"pa{t}") for t in range(PACK)]
        nbs = [sb.tile([P, W], F32, name=f"nb{t}") for t in range(PACK)]

        def differences(t):
            y = stair.tile([P, S], F32, name=f"y{t}", offset=4 * W * t)
            if t == 0:
                for bank, cols in zip(y0_banks, halves):
                    nc.scalar.copy(y[:, cols], bank[:])
            else:
                nc.scalar.copy(y[:], y_banks[t][:])
            nc.scalar.activation(pas[t][:], y[:].indirect(n1_t[:]), ACT.Copy)
            nc.scalar.activation(nbs[t][:], y[:].indirect(n2_t[:]), ACT.Copy, scale=-1.0)
            nc.vector.tensor_tensor(z_tiles[t][:].indirect(n2_t[:]), pas[t][:], nbs[t][:], ALU.add)

        def sums(t):
            if t < PACK - 1:
                pa75 = stair.tile([P, W], F32, name=f"pa75{t}", offset=4 * W * (t + 1))
            else:
                pa75 = sb.tile([P, W], F32, name=f"pa75{t}")
            pb75 = sb.tile([P, W], F32, name=f"pb75{t}")
            nc.scalar.activation(pa75[:], pas[t][:], ACT.Copy, scale=0.75)
            nc.scalar.activation(pb75[:], nbs[t][:], ACT.Copy, scale=-0.75)
            nc.vector.tensor_tensor(z_tiles[t][:].indirect(n1_t[:]), pa75[:], pb75[:], ALU.add)

        differences(0)
        for t in range(1, PACK):
            differences(t)
            sums(t - 1)
        sums(PACK - 1)

        h0_banks = [
            psum.tile([P, S // 2], F32, name="h0_left", tag="bank_a"),
            psum.tile([P, S // 2], F32, name="h0_right", tag="bank_b"),
        ]
        h_banks = [None] + [psum.tile([P, S], F32, name=f"h_bank{t}") for t in range(1, PACK)]
        for bank, cols in zip(h0_banks, halves):
            product(bank[:], 2, 0, hz_codes[:, cols], hz_scales[:, cols], True, False)
        for t in range(1, PACK):
            product(h_banks[t][:], 2, t, hz_codes[:], hz_scales[:], True, False)

        def quantise(planes, name):
            grouped = sb.tile([P, S, PACK], BF16, name=f"{name}_grouped", align_bytes=64)
            codes = sb.tile([P, S], U32, name=f"{name}_codes", align_bytes=64)
            scales = sb.tile([P, S], U8, name=f"{name}_scales", align_bytes=64)
            interleave(nc.vector.tensor_copy, grouped, planes, 0, S // 2)
            interleave(nc.scalar.copy, grouped, planes, SPLIT, S)
            interleave(nc.vector.tensor_copy, grouped, planes, S // 2, SPLIT)
            for cols in halves:
                nc.vector.quantize_mx(
                    out=codes[:, cols].bitcast(FP8X4),
                    scales=scales[:, cols],
                    in_=grouped[:, cols, :].rearrange("p c t -> p (c t)"),
                )
            return codes, scales

        z_planes = stair.tile([P, PACK, S], BF16, name="z_planes", offset=4 * W * PACK, align_bytes=64)
        for t in range(PACK - 1):
            nc.scalar.activation(z_planes[:, t, :], z_tiles[t][:], ACT.Copy, scale=gain[:, t : t + 1])
        last = PACK - 1
        last_gain = gain[:, last : last + 1]
        nc.vector.tensor_scalar_mul(z_planes[:, last, 0 : S // 2], z_tiles[last][:, 0 : S // 2], last_gain)
        nc.scalar.activation(z_planes[:, last, SPLIT:S], z_tiles[last][:, SPLIT:S], ACT.Copy, scale=last_gain)
        nc.vector.tensor_scalar_mul(z_planes[:, last, S // 2 : SPLIT], z_tiles[last][:, S // 2 : SPLIT], last_gain)
        z_codes, z_scales = quantise(z_planes, "z")
        for bank, cols in zip(h0_banks, halves):
            product(bank[:], 1, 0, z_codes[:, cols], z_scales[:, cols], False, True)
        for t in range(1, PACK):
            product(h_banks[t][:], 1, t, z_codes[:], z_scales[:], False, True)

        out_rows = out_0.rearrange("(p t) c -> p t c", t=PACK)
        h_tiles = [sb.tile([P, S], F32, name=f"h{t}") for t in range(PACK)]
        roots, parts = [], []
        for t in range(PACK):
            h = h_tiles[t]
            h_abs = sb.tile([P, S], F32, name=f"h_abs{t}", tag="h_abs", align_bytes=64)
            if t == 0:
                for bank, cols in zip(h0_banks, halves):
                    nc.scalar.activation(h_abs[:, cols], bank[:], ACT.Abs)
                    nc.vector.tensor_copy(h[:, cols], bank[:])
            else:
                nc.vector.tensor_copy(h[:], h_banks[t][:])
                nc.scalar.activation(h_abs[:], h_banks[t][:], ACT.Abs)
            size = sb.tile([P, G], F32, name=f"size{t}", tag=f"size{t}")
            root = sb.tile([P, G], F32, name=f"root{t}")
            nc.scalar.activation(size[:], h_abs[:].indirect(n4_t[:]), ACT.Copy)
            nc.scalar.activation(root[:], size[:], ACT.Abs_reciprocal_sqrt, bias=half[:])
            part = sb.tile([P, G], F32, name=f"part{t}")
            if t == 3:
                ra2 = sb.tile([P, G], F32, name="ra2", tag="size3")
                nc.vector.tensor_tensor(ra2[:], parts[2][:], roots[2][:], ALU.mult)
            nc.vector.tensor_tensor(part[:], h[:].indirect(n3_t[:]), root[:], ALU.mult)
            if t != 2:
                nc.vector.tensor_tensor(h[:].indirect(n3_t[:]), part[:], root[:], ALU.mult)
                nc.sync.dma_start(out_rows[:, t, :], h[:])
            roots.append(root)
            parts.append(part)
        o_planes = sb.tile([P, PACK, S], BF16, name="o_planes", tag="h_abs", align_bytes=64)
        for t in range(2):
            nc.scalar.copy(o_planes[:, t, :], h_tiles[t][:])
        nc.scalar.activation(h_tiles[2][:].indirect(n3_t[:]), ra2[:], ACT.Copy)
        nc.sync.dma_start(out_rows[:, 2, :], h_tiles[2][:])
        nc.scalar.copy(o_planes[:, 2, :], h_tiles[2][:])
        nc.vector.tensor_copy(o_planes[:, PACK - 1, :], h_tiles[PACK - 1][:])
        o_codes, o_scales = quantise(o_planes, "o")
        out_words = out_1[0].rearrange("p c r -> p (c r)").bitcast(I32)
        for cols in halves:
            nc.sync.dma_start(out_words[:, cols], o_codes[:, cols].bitcast(I32))
        out_scale_rows = out_2[0].bitcast(I32)
        for q in range(4):
            queue = nc.sync if q < 2 else nc.scalar
            queue.dma_start(out_scale_rows[4 * q : 4 * q + 4, :], o_scales[:].bitcast(I32)[32 * q : 32 * q + 4, :])
